import numpy as np
import ml_dtypes


def mxq(x, axis, fmt="e4m3"):
    dtype, down = {"e4m3": (ml_dtypes.float8_e4m3fn, 7), "e5m2": (ml_dtypes.float8_e5m2, 14)}[fmt]
    v = np.moveaxis(np.asarray(x, np.float32).astype(ml_dtypes.bfloat16).astype(np.float64), axis, -1)
    blocks = v.reshape(v.shape[:-1] + (-1, 32))
    amax = np.abs(blocks).max(-1, keepdims=True)
    byte = np.maximum(np.where(amax > 0, np.frexp(amax)[1] - 1 + 127, 0) - down, 1)
    scale = np.exp2(byte - 127.0)
    codes = (blocks / scale).astype(np.float32).astype(dtype).astype(np.float64)
    return np.moveaxis((codes * scale).reshape(v.shape), -1, axis)


WIDE = False


def mx_kscale(k):
    if not WIDE:
        return np.ones(k)
    levels = np.array([30, -30])
    if k % 512:
        return np.exp2(np.random.permutation(np.resize(levels, k // 32))).repeat(32)
    a = np.empty((k // 512, 16))
    for p in range(k // 512):
        a[p, :8] = np.random.permutation(np.resize(levels, 8))
        for g in range(8):
            far = levels[np.abs(levels - a[p, g]) >= 10]
            a[p, g + 8] = far[np.random.randint(len(far))]
    return np.exp2(a.ravel()).repeat(32)


def f64(x):
    return np.asarray(x).astype(np.float64)


def striped(idx):
    return np.tile(np.asarray(idx).reshape(-1, 16).T, (8, 1)).astype(np.uint16)


def unstriped(offs):
    return offs[:16].T.reshape(-1).astype(np.int64)


def striped8(idx):
    return np.asarray(idx).reshape(8, -1, 16).transpose(0, 2, 1).reshape(128, -1).astype(np.uint16)


def unstriped8(offs):
    return offs.reshape(8, 16, -1).transpose(0, 2, 1).reshape(8, -1).astype(np.int64)


def pick8(x, idx, run):
    r = np.arange(len(x))
    return x[r[:, None], idx[r % (8 * run) // run]]


E2M1 = np.array([0.0, 0.5, 1.0, 1.5, 2.0, 3.0, 4.0, 6.0, -0.0, -0.5, -1.0, -1.5, -2.0, -3.0, -4.0, -6.0])


def pack_weight(w, fmt):
    k, n = w.shape
    w = f64(np.asarray(w, np.float32).astype(ml_dtypes.bfloat16)).reshape(k // 32, 32, n)
    amax = np.abs(w).max(1)
    if fmt in ("e4m3", "e5m2"):
        byte = np.frexp(amax)[1] - 1 + 127 - (7 if fmt == "e4m3" else 14)
    else:
        mant, ex = np.frexp(amax / 6.0)
        byte = np.where(mant > 0.5, ex, ex - 1) + 127
    byte = np.clip(np.where(amax > 0, byte, 1), 1, 254)
    scaled = (w * np.exp2(127.0 - byte)[:, None, :]).reshape(k, n).astype(np.float32)
    by_word = np.ascontiguousarray(scaled.reshape(k // 512, 128, 4, n).transpose(0, 1, 3, 2))
    if fmt in ("e4m3", "e5m2"):
        words = by_word.astype(ml_dtypes.float8_e4m3fn if fmt == "e4m3" else ml_dtypes.float8_e5m2).view(np.uint8)
    else:
        c = by_word.astype(ml_dtypes.float4_e2m1fn).view(np.uint8) & 0xF
        words = (c[..., 0::2] | (c[..., 1::2] << 4)).reshape(k // 512, 128, 2 * n)
    return np.ascontiguousarray(words), np.ascontiguousarray(byte.astype(np.uint8).reshape(k // 512, 16, n))


def unpack_weight(words, scales, fmt):
    g, _, n = scales.shape
    words = np.ascontiguousarray(words).reshape(g, 128, n, -1)
    if fmt in ("e4m3", "e5m2"):
        vals = words.view(ml_dtypes.float8_e4m3fn if fmt == "e4m3" else ml_dtypes.float8_e5m2).astype(np.float64)
    else:
        nib = np.empty((g, 128, n, 4), np.uint8)
        nib[..., 0::2] = words & 0xF
        nib[..., 1::2] = words >> 4
        vals = E2M1[nib]
    vals = vals * np.repeat(np.exp2(scales.astype(np.float64) - 127.0), 8, axis=1)[..., None]
    return vals.transpose(0, 1, 3, 2).reshape(g * 512, n)


K, T, J, R, V, C, D, O, N, E = 512, 1024, 256, 512, 1024, 512, 512, 256, 256, 512


def setup_inputs():
    n = np.random.standard_normal
    idx = np.random.permutation(V)[:R]
    idx2 = np.random.permutation(T)[:J]
    idx3 = np.stack([np.random.permutation(C)[:J] for _ in range(8)])
    idx4 = np.stack([np.random.permutation(D)[:J] for _ in range(8)])
    idx5 = np.random.permutation(C)[:O]
    idx6 = np.random.permutation(D)[:O]
    idx7 = np.stack([np.random.permutation(E)[:O] for _ in range(8)])
    fk = mx_kscale(K)
    fr = mx_kscale(R)
    tr = np.ones(V)
    tr[idx] = fr
    xtp = pack_weight(n((K, T)) / fk[:, None], "e5m2")
    wtp = pack_weight(n((K, V)) * 1 / np.sqrt(K) * fk[:, None] * tr, "e2m1")
    w2p = pack_weight(n((K, R)) * 1 / np.sqrt(K) * fk[:, None] * fr, "e4m3")
    wbp = pack_weight(n((R, N)) * 1 / np.sqrt(R) / fr[:, None], "e2m1")
    return {
        "xt_words": xtp[0],
        "xt_scales": xtp[1],
        "wt_words": wtp[0],
        "wt_scales": wtp[1],
        "w2_words": w2p[0],
        "w2_scales": w2p[1],
        "sa": (np.random.uniform(0.5, 1.6, (R, 1))).astype(np.float32),
        "sb": (np.random.uniform(0.5, 1.6, (R, 1))).astype(np.float32),
        "wb_words": wbp[0],
        "wb_scales": wbp[1],
        "offs": striped(idx),
        "offs2": striped(idx2),
        "offs3": striped8(idx3),
        "offs4": striped8(idx4),
        "offs5": striped(idx5),
        "offs6": striped(idx6),
        "offs7": striped8(idx7),
    }


def reference(xt_words, xt_scales, wt_words, wt_scales, w2_words, w2_scales, sa, sb, wb_words, wb_scales, offs, offs2, offs3, offs4, offs5, offs6, offs7):
    idx = unstriped(offs)
    idx2 = unstriped(offs2)
    idx3 = unstriped8(offs3)
    idx4 = unstriped8(offs4)
    idx5 = unstriped(offs5)
    idx6 = unstriped(offs6)
    idx7 = unstriped8(offs7)
    xtu = unpack_weight(xt_words, xt_scales, "e5m2")
    wtu = unpack_weight(wt_words, wt_scales, "e2m1")
    w2u = unpack_weight(w2_words, w2_scales, "e4m3")
    wbu = unpack_weight(wb_words, wb_scales, "e2m1")
    wtidxg = wtu[:, idx]
    xtidx2g = xtu[:, idx2]
    a = wtidxg.T @ xtidx2g
    b = w2u.T @ xtidx2g
    pw = np.zeros((R, C))
    pw[np.arange(R)[:, None], idx3[np.arange(R) % 512 // 64]] = a
    pv = np.zeros((R, D))
    pv[np.arange(R)[:, None], idx4[np.arange(R) % 512 // 64]] = b
    hid = np.abs(pw[:, idx5] * f64(sa) - pv[:, idx6] * f64(sb))
    hidq = mxq(hid, 0, "e4m3")
    p = wbu.T @ hidq
    y = np.zeros((N, E))
    y[np.arange(N)[:, None], idx7[np.arange(N) % 128 // 16]] = p
    return y

@@ -1,0 +1,195 @@
+from contextlib import ExitStack
+
+import concourse.mybir as mybir
+
+K, T, J, R, V, C, O, N, E = 512, 1024, 256, 512, 1024, 512, 256, 256, 512
+FLOPS = 2 * K * R * J * 2 + 2 * R * N * O
+
+F32 = mybir.dt.float32
+BF16 = mybir.dt.bfloat16
+I32 = mybir.dt.int32
+U32 = mybir.dt.uint32
+U16 = mybir.dt.uint16
+U8 = mybir.dt.uint8
+E4M3 = mybir.dt.float8_e4m3fn_x4
+E5M2 = mybir.dt.float8_e5m2_x4
+E2M1 = mybir.dt.float4_e2m1fn_x4
+COPY = mybir.ActivationFunctionType.Copy
+ALU = mybir.AluOpType
+
+P = 128
+PACK = 4
+QUADS = 4
+HALF = O // 2
+ALIGN = 64
+
+
+def tile_list_twoownboards_storeleads_one_ownpage_kernel(
+    tc, xt_words, xt_scales, wt_words, wt_scales, w2_words, w2_scales, sa, sb, wb_words, wb_scales,
+    offs, offs2, offs3, offs4, offs5, offs6, offs7, out,
+):
+    nc = tc.nc
+    with ExitStack() as ctx:
+        lists = ctx.enter_context(tc.tile_pool(name="lists", bufs=1))
+        pool = ctx.enter_context(tc.tile_pool(name="work", bufs=1))
+        psum = ctx.enter_context(tc.psum_pool(name="psum", bufs=4))
+
+        def tile(shape, dtype, name, tag=None):
+            return pool.tile(shape, dtype, name=name, tag=tag or name, align_bytes=ALIGN)
+
+        def load_list(src, name):
+            held = lists.tile(list(src.shape), U16, name=name)
+            nc.sync.dma_start(held[:], src)
+            return held
+
+        def zeroed_plane(width, name, engine=nc.vector):
+            plane = tile([P, width], U8, name)
+            engine.memset(plane[:].bitcast(I32), 0)
+            return plane
+
+        def load_rows(queue, plane, scales):
+            for q in range(QUADS):
+                queue.dma_start(plane[32 * q : 32 * q + 4, :].bitcast(I32), scales[0, 4 * q : 4 * q + 4, :].bitcast(I32))
+
+        def stage_rows(queue, scales, name, tag=None):
+            width = scales.shape[2] // 4
+            staged = tile([4, QUADS * width], I32, name, tag)
+            queue.dma_start(
+                staged[:].rearrange("r (q n) -> r q n", q=QUADS),
+                scales[0].bitcast(I32).rearrange("(q r) n -> r q n", r=4),
+            )
+            return staged
+
+        def spread_rows(plane, staged):
+            width = staged.shape[1] // QUADS
+            for q in range(QUADS):
+                nc.vector.tensor_copy(plane[32 * q : 32 * q + 4, :].bitcast(I32), staged[:, q * width : (q + 1) * width])
+
+        def deal(dst, src, t0, t1, copy=nc.vector.tensor_copy):
+            copy(
+                dst[:, t0 * P : t1 * P].rearrange("p (t m) -> p t m", m=P),
+                src[:].rearrange("p (m t) -> p t m", t=PACK)[:, t0:t1, :],
+            )
+
+        def zeroed_board(name, tag=None):
+            board = tile([P, C], F32, name, tag)
+            nc.gpsimd.memset(board[:], 0.0)
+            return board
+
+        xt_plane = zeroed_plane(T, "xt_plane")
+        w2_plane = zeroed_plane(R, "w2_plane")
+        tok = load_list(offs2, "tok")
+        xt_staged = tile([P, T // 2], I32, "xt_staged")
+        for u in range(2):
+            nc.sync.dma_start(
+                xt_staged[64 * u : 64 * u + 4, :].rearrange("r (q n) -> r q n", q=2),
+                xt_scales[0, 8 * u : 8 * u + 8, :].bitcast(I32).rearrange("(q r) n -> r q n", r=4),
+            )
+        xt_w = tile([P, T], U32, "xt_w")
+        nc.sync.dma_start(xt_w[:].bitcast(I32), xt_words[0].rearrange("p n t -> p (n t)").bitcast(I32))
+        w2_w = tile([P, R], U32, "w2_w")
+        nc.sync.dma_start(w2_w[:].bitcast(I32), w2_words[0].rearrange("p n t -> p (n t)").bitcast(I32))
+        w2_staged = stage_rows(nc.scalar, w2_scales, "w2_staged")
+        put_b = load_list(offs4, "put_b")
+        ent = load_list(offs, "ent")
+        put_a = load_list(offs3, "put_a")
+        pick_w = load_list(offs5, "pick_w")
+        pick_v = load_list(offs6, "pick_v")
+        put_p = load_list(offs7, "put_p")
+        pv = [zeroed_board("pv%d" % t) for t in range(PACK)]
+
+        for q in range(QUADS):
+            nc.vector.tensor_copy(
+                xt_plane[32 * q : 32 * q + 4, :].bitcast(I32),
+                xt_staged[64 * (q // 2) : 64 * (q // 2) + 4, (q % 2) * T // 4 : (q % 2 + 1) * T // 4],
+            )
+        x_s = tile([P, J], U8, "x_s")
+        nc.vector.tensor_copy(x_s[:], xt_plane[:].indirect(tok[:]))
+        spread_rows(w2_plane, w2_staged)
+        w2d_s = tile([P, R], U8, "w2d_s")
+        deal(w2d_s, w2_plane, 0, 1)
+        x_w = tile([P, J], U32, "x_w")
+        nc.vector.tensor_copy(x_w[:], xt_w[:].indirect(tok[:]))
+        w2d_w = tile([P, R], U32, "w2d_w")
+        deal(w2d_w, w2_w, 0, 1, nc.scalar.copy)
+
+        def product(words, scales, fmt, t, board, put, name):
+            cols = slice(t * P, (t + 1) * P)
+            acc = psum.tile([P, J], F32, name="acc")
+            nc.tensor.matmul_mx(
+                acc[:], lhsT=words[:, cols].bitcast(fmt), lhsT_scale=scales[:, cols],
+                rhs=x_w[:].bitcast(E5M2), rhs_scale=x_s[:], start=True, stop=True,
+            )
+            sums = tile([P, J], F32, name)
+            nc.vector.tensor_copy(sums[:], acc[:])
+            nc.scalar.activation(board[:].indirect(put[:]), sums[:], COPY)
+
+        product(w2d_w, w2d_s, E4M3, 0, pv[0], put_b, "b0")
+        deal(w2d_s, w2_plane, 1, PACK)
+        deal(w2d_w, w2_w, 1, PACK)
+        for t in range(1, PACK):
+            product(w2d_w, w2d_s, E4M3, t, pv[t], put_b, "b%d" % t)
+
+        wt_plane = zeroed_plane(V, "wt_plane")
+        wb_s = zeroed_plane(N, "wb_s")
+        wb_w = tile([P, N], U16, "wb_w")
+        nc.sync.dma_start(wb_w[:].bitcast(I32), wb_words[0].bitcast(I32))
+        load_rows(nc.sync, wb_s, wb_scales)
+        wt_staged = stage_rows(nc.sync, wt_scales, "wt_staged", "xt_w")
+        wt_w = tile([P, V], U16, "wt_w", "w2_w")
+        nc.sync.dma_start(wt_w[:].bitcast(I32), wt_words[0].bitcast(I32))
+        spread_rows(wt_plane, wt_staged)
+        e_s = tile([P, R], U8, "e_s")
+        nc.vector.tensor_copy(e_s[:], wt_plane[:].indirect(ent[:]))
+        e_w = tile([P, R], U16, "e_w")
+        nc.vector.tensor_copy(e_w[:], wt_w[:].indirect(ent[:]))
+        ed_s = tile([P, R], U8, "ed_s")
+        ed_w = tile([P, R], U16, "ed_w")
+        pw = [zeroed_board("pw%d" % t, "b%d" % t) for t in range(PACK)]
+        deal(ed_s, e_s, 0, 1)
+        deal(ed_w, e_w, 0, 1)
+        product(ed_w, ed_s, E2M1, 0, pw[0], put_a, "a0")
+        deal(ed_s, e_s, 1, PACK)
+        deal(ed_w, e_w, 1, PACK)
+        for t in range(1, PACK):
+            product(ed_w, ed_s, E2M1, t, pw[t], put_a, "a%d" % t)
+
+        gains = tile([P, 16], F32, "gains", "a0")
+        nc.sync.dma_start(gains[:, 0:PACK], sa.rearrange("(p t) o -> p (t o)", t=PACK))
+        nc.sync.dma_start(gains[:, 8 : 8 + PACK], sb.rearrange("(p t) o -> p (t o)", t=PACK))
+        pages = [zeroed_board("page%d" % c, "a%d" % (c + 1)) for c in range(N // P)]
+
+        def hidden(h):
+            cols = slice(h * HALF // 16, (h + 1) * HALF // 16)
+            gw = tile([P, PACK, HALF], F32, "gw%d" % h)
+            gv = tile([P, PACK, HALF], F32, "gv%d" % h)
+            diff = tile([P, PACK, HALF], F32, "diff%d" % h)
+            hid = tile([P, HALF, PACK], BF16, "hid%d" % h)
+            for t in range(PACK):
+                nc.scalar.activation(gv[:, t, :], pv[t][:].indirect(pick_v[:, cols]), COPY, scale=gains[:, 8 + t : 9 + t])
+                nc.scalar.activation(gw[:, t, :], pw[t][:].indirect(pick_w[:, cols]), COPY, scale=gains[:, t : t + 1])
+                nc.vector.tensor_tensor(diff[:, t, :], gw[:, t, :], gv[:, t, :], ALU.subtract)
+                if t % 2 == 1:
+                    pair = diff[:, t - 1 : t + 1, :].rearrange("p t o -> p o t")
+                    nc.vector.scalar_tensor_tensor(hid[:, :, t - 1 : t + 1], pair, -1.0, pair, ALU.mult, ALU.max)
+            h_w = tile([P, HALF], U32, "h_w%d" % h)
+            h_s = tile([P, HALF], U8, "h_s%d" % h)
+            nc.vector.quantize_mx(h_w[:].bitcast(E4M3), h_s[:], hid[:].rearrange("p o t -> p (o t)"))
+            results = []
+            for c in range(N // P):
+                acc = psum.tile([P, HALF], F32, name="acc_p")
+                nc.tensor.matmul_mx(
+                    acc[:], lhsT=wb_w[:, c * P : (c + 1) * P].bitcast(E2M1), lhsT_scale=wb_s[:, c * P : (c + 1) * P],
+                    rhs=h_w[:].bitcast(E4M3), rhs_scale=h_s[:], start=True, stop=True,
+                )
+                sums = tile([P, HALF], F32, "p%d%d" % (h, c))
+                nc.vector.tensor_copy(sums[:], acc[:])
+                results.append(sums)
+            return results
+
+        halves = [hidden(h) for h in range(2)]
+        for h in range(2):
+            for c in range(N // P):
+                nc.scalar.activation(pages[c][:].indirect(put_p[:, h * HALF // 16 : (h + 1) * HALF // 16]), halves[h][c][:], COPY)
+        for c in range(N // P):
+            nc.sync.dma_start(out[c * P : (c + 1) * P, :], pages[c][:])

@@ -42,28 +42,33 @@ def tile_list_twoownboards_storeleads_one_ownpage_kernel(
             nc.sync.dma_start(held[:], src)
             return held
 
-        def zeroed_plane(width, name, engine=nc.vector):
+        def zeroed_plane(width, name):
             plane = tile([P, width], U8, name)
-            engine.memset(plane[:].bitcast(I32), 0)
+            nc.vector.memset(plane[:].bitcast(I32), 0)
             return plane
 
         def load_rows(queue, plane, scales):
             for q in range(QUADS):
                 queue.dma_start(plane[32 * q : 32 * q + 4, :].bitcast(I32), scales[0, 4 * q : 4 * q + 4, :].bitcast(I32))
 
-        def stage_rows(queue, scales, name, tag=None):
-            width = scales.shape[2] // 4
-            staged = tile([4, QUADS * width], I32, name, tag)
-            queue.dma_start(
-                staged[:].rearrange("r (q n) -> r q n", q=QUADS),
-                scales[0].bitcast(I32).rearrange("(q r) n -> r q n", r=4),
-            )
+        def stage_rows(queue, scales, name):
+            words = scales.shape[2] // 4
+            staged = tile([P, 2 * words], I32, name)
+            for u in range(2):
+                queue.dma_start(
+                    staged[64 * u : 64 * u + 4, :].rearrange("r (q n) -> r q n", q=2),
+                    scales[0, 8 * u : 8 * u + 8, :].bitcast(I32).rearrange("(q r) n -> r q n", r=4),
+                )
             return staged
 
         def spread_rows(plane, staged):
-            width = staged.shape[1] // QUADS
+            words = staged.shape[1] // 2
             for q in range(QUADS):
-                nc.vector.tensor_copy(plane[32 * q : 32 * q + 4, :].bitcast(I32), staged[:, q * width : (q + 1) * width])
+                first = 64 * (q // 2)
+                nc.vector.tensor_copy(
+                    plane[32 * q : 32 * q + 4, :].bitcast(I32),
+                    staged[first : first + 4, (q % 2) * words : (q % 2 + 1) * words],
+                )
 
         def deal(dst, src, t0, t1, copy=nc.vector.tensor_copy):
             copy(
@@ -71,20 +76,15 @@ def tile_list_twoownboards_storeleads_one_ownpage_kernel(
                 src[:].rearrange("p (m t) -> p t m", t=PACK)[:, t0:t1, :],
             )
 
-        def zeroed_board(name, tag=None):
+        def zeroed_board(engine, name, tag=None):
             board = tile([P, C], F32, name, tag)
-            nc.gpsimd.memset(board[:], 0.0)
+            engine.memset(board[:], 0.0)
             return board
 
         xt_plane = zeroed_plane(T, "xt_plane")
         w2_plane = zeroed_plane(R, "w2_plane")
         tok = load_list(offs2, "tok")
-        xt_staged = tile([P, T // 2], I32, "xt_staged")
-        for u in range(2):
-            nc.sync.dma_start(
-                xt_staged[64 * u : 64 * u + 4, :].rearrange("r (q n) -> r q n", q=2),
-                xt_scales[0, 8 * u : 8 * u + 8, :].bitcast(I32).rearrange("(q r) n -> r q n", r=4),
-            )
+        xt_staged = stage_rows(nc.sync, xt_scales, "xt_staged")
         xt_w = tile([P, T], U32, "xt_w")
         nc.sync.dma_start(xt_w[:].bitcast(I32), xt_words[0].rearrange("p n t -> p (n t)").bitcast(I32))
         w2_w = tile([P, R], U32, "w2_w")
@@ -96,13 +96,9 @@ def tile_list_twoownboards_storeleads_one_ownpage_kernel(
         pick_w = load_list(offs5, "pick_w")
         pick_v = load_list(offs6, "pick_v")
         put_p = load_list(offs7, "put_p")
-        pv = [zeroed_board("pv%d" % t) for t in range(PACK)]
+        pv = [zeroed_board(nc.gpsimd, "pv%d" % t) for t in range(PACK)]
 
-        for q in range(QUADS):
-            nc.vector.tensor_copy(
-                xt_plane[32 * q : 32 * q + 4, :].bitcast(I32),
-                xt_staged[64 * (q // 2) : 64 * (q // 2) + 4, (q % 2) * T // 4 : (q % 2 + 1) * T // 4],
-            )
+        spread_rows(xt_plane, xt_staged)
         x_s = tile([P, J], U8, "x_s")
         nc.vector.tensor_copy(x_s[:], xt_plane[:].indirect(tok[:]))
         spread_rows(w2_plane, w2_staged)
@@ -131,33 +127,34 @@ def tile_list_twoownboards_storeleads_one_ownpage_kernel(
             product(w2d_w, w2d_s, E4M3, t, pv[t], put_b, "b%d" % t)
 
         wt_plane = zeroed_plane(V, "wt_plane")
+        load_rows(nc.sync, wt_plane, wt_scales)
+        wt_w = tile([P, V], U16, "wt_w")
+        nc.sync.dma_start(wt_w[:].bitcast(I32), wt_words[0].bitcast(I32))
         wb_s = zeroed_plane(N, "wb_s")
         wb_w = tile([P, N], U16, "wb_w")
         nc.sync.dma_start(wb_w[:].bitcast(I32), wb_words[0].bitcast(I32))
         load_rows(nc.sync, wb_s, wb_scales)
-        wt_staged = stage_rows(nc.sync, wt_scales, "wt_staged", "xt_w")
-        wt_w = tile([P, V], U16, "wt_w", "w2_w")
-        nc.sync.dma_start(wt_w[:].bitcast(I32), wt_words[0].bitcast(I32))
-        spread_rows(wt_plane, wt_staged)
-        e_s = tile([P, R], U8, "e_s")
+        e_s = tile([P, R], U8, "e_s", "w2d_s")
         nc.vector.tensor_copy(e_s[:], wt_plane[:].indirect(ent[:]))
-        e_w = tile([P, R], U16, "e_w")
+        e_w = tile([P, R], U16, "e_w", "w2d_w")
         nc.vector.tensor_copy(e_w[:], wt_w[:].indirect(ent[:]))
         ed_s = tile([P, R], U8, "ed_s")
         ed_w = tile([P, R], U16, "ed_w")
-        pw = [zeroed_board("pw%d" % t, "b%d" % t) for t in range(PACK)]
+        pw = [zeroed_board(nc.gpsimd, "pw0"), zeroed_board(nc.vector, "pw1")]
         deal(ed_s, e_s, 0, 1)
         deal(ed_w, e_w, 0, 1)
         product(ed_w, ed_s, E2M1, 0, pw[0], put_a, "a0")
         deal(ed_s, e_s, 1, PACK)
         deal(ed_w, e_w, 1, PACK)
+        pw.append(zeroed_board(nc.gpsimd, "pw2", "w2d_s"))
+        pw.append(zeroed_board(nc.gpsimd, "pw3", "w2d_w"))
         for t in range(1, PACK):
             product(ed_w, ed_s, E2M1, t, pw[t], put_a, "a%d" % t)
 
         gains = tile([P, 16], F32, "gains", "a0")
         nc.sync.dma_start(gains[:, 0:PACK], sa.rearrange("(p t) o -> p (t o)", t=PACK))
         nc.sync.dma_start(gains[:, 8 : 8 + PACK], sb.rearrange("(p t) o -> p (t o)", t=PACK))
-        pages = [zeroed_board("page%d" % c, "a%d" % (c + 1)) for c in range(N // P)]
+        pages = [zeroed_board(nc.gpsimd, "page%d" % c, "a%d" % (c + 1)) for c in range(N // P)]
 
         def hidden(h):
             cols = slice(h * HALF // 16, (h + 1) * HALF // 16)

@@ -96,33 +96,37 @@ def tile_list_twoownboards_storeleads_one_ownpage_kernel(
         pick_w = load_list(offs5, "pick_w")
         pick_v = load_list(offs6, "pick_v")
         put_p = load_list(offs7, "put_p")
-        pv = [zeroed_board(nc.gpsimd, "pv%d" % t) for t in range(PACK)]
+        pv = [zeroed_board(nc.gpsimd if t < 2 else nc.vector, "pv%d" % t) for t in range(PACK - 1)]
 
         spread_rows(xt_plane, xt_staged)
-        x_s = tile([P, J], U8, "x_s")
-        nc.vector.tensor_copy(x_s[:], xt_plane[:].indirect(tok[:]))
         spread_rows(w2_plane, w2_staged)
-        w2d_s = tile([P, R], U8, "w2d_s")
-        deal(w2d_s, w2_plane, 0, 1)
+        x_s = tile([P, J], U8, "x_s")
         x_w = tile([P, J], U32, "x_w")
-        nc.vector.tensor_copy(x_w[:], xt_w[:].indirect(tok[:]))
+        w2d_s = tile([P, R], U8, "w2d_s")
         w2d_w = tile([P, R], U32, "w2d_w")
-        deal(w2d_w, w2_w, 0, 1, nc.scalar.copy)
 
-        def product(words, scales, fmt, t, board, put, name):
+        def product(words, scales, fmt, t, board, put, name, j0=0, j1=J):
             cols = slice(t * P, (t + 1) * P)
-            acc = psum.tile([P, J], F32, name="acc")
+            acc = psum.tile([P, j1 - j0], F32, name="acc")
             nc.tensor.matmul_mx(
                 acc[:], lhsT=words[:, cols].bitcast(fmt), lhsT_scale=scales[:, cols],
-                rhs=x_w[:].bitcast(E5M2), rhs_scale=x_s[:], start=True, stop=True,
+                rhs=x_w[:, j0:j1].bitcast(E5M2), rhs_scale=x_s[:, j0:j1], start=True, stop=True,
             )
-            sums = tile([P, J], F32, name)
+            sums = tile([P, j1 - j0], F32, name)
             nc.vector.tensor_copy(sums[:], acc[:])
-            nc.scalar.activation(board[:].indirect(put[:]), sums[:], COPY)
+            nc.scalar.activation(board[:].indirect(put[:, j0 // 16 : j1 // 16]), sums[:], COPY)
 
-        product(w2d_w, w2d_s, E4M3, 0, pv[0], put_b, "b0")
+        deal(w2d_w, w2_w, 0, 1, nc.scalar.copy)
+        deal(w2d_w, w2_w, 1, PACK, nc.scalar.copy)
+        for j0 in (0, J // 2):
+            j1 = j0 + J // 2
+            nc.vector.tensor_copy(x_s[:, j0:j1], xt_plane[:].indirect(tok[:, j0 // 16 : j1 // 16]))
+            if j0 == 0:
+                deal(w2d_s, w2_plane, 0, 1)
+            nc.vector.tensor_copy(x_w[:, j0:j1], xt_w[:].indirect(tok[:, j0 // 16 : j1 // 16]))
+            product(w2d_w, w2d_s, E4M3, 0, pv[0], put_b, "b0_%d" % j0, j0, j1)
         deal(w2d_s, w2_plane, 1, PACK)
-        deal(w2d_w, w2_w, 1, PACK)
+        pv.append(zeroed_board(nc.gpsimd, "pv3", "w2_w"))
         for t in range(1, PACK):
             product(w2d_w, w2d_s, E4M3, t, pv[t], put_b, "b%d" % t)
 
@@ -140,7 +144,7 @@ def tile_list_twoownboards_storeleads_one_ownpage_kernel(
         nc.vector.tensor_copy(e_w[:], wt_w[:].indirect(ent[:]))
         ed_s = tile([P, R], U8, "ed_s")
         ed_w = tile([P, R], U16, "ed_w")
-        pw = [zeroed_board(nc.gpsimd, "pw0"), zeroed_board(nc.vector, "pw1")]
+        pw = [zeroed_board(nc.gpsimd, "pw0", "w2_plane"), zeroed_board(nc.gpsimd, "pw1", "b1")]
         deal(ed_s, e_s, 0, 1)
         deal(ed_w, e_w, 0, 1)
         product(ed_w, ed_s, E2M1, 0, pw[0], put_a, "a0")

@@ -83,20 +83,20 @@ def tile_list_twoownboards_storeleads_one_ownpage_kernel(
 
         xt_plane = zeroed_plane(T, "xt_plane")
         w2_plane = zeroed_plane(R, "w2_plane")
-        tok = load_list(offs2, "tok")
         xt_staged = stage_rows(nc.sync, xt_scales, "xt_staged")
+        w2_staged = stage_rows(nc.sync, w2_scales, "w2_staged")
+        tok = load_list(offs2, "tok")
         xt_w = tile([P, T], U32, "xt_w")
         nc.sync.dma_start(xt_w[:].bitcast(I32), xt_words[0].rearrange("p n t -> p (n t)").bitcast(I32))
         w2_w = tile([P, R], U32, "w2_w")
         nc.sync.dma_start(w2_w[:].bitcast(I32), w2_words[0].rearrange("p n t -> p (n t)").bitcast(I32))
-        w2_staged = stage_rows(nc.scalar, w2_scales, "w2_staged")
         put_b = load_list(offs4, "put_b")
         ent = load_list(offs, "ent")
         put_a = load_list(offs3, "put_a")
         pick_w = load_list(offs5, "pick_w")
         pick_v = load_list(offs6, "pick_v")
         put_p = load_list(offs7, "put_p")
-        pv = [zeroed_board(nc.gpsimd if t < 2 else nc.vector, "pv%d" % t) for t in range(PACK - 1)]
+        pv = [zeroed_board(nc.gpsimd if t < 1 else nc.vector, "pv%d" % t) for t in range(PACK - 1)]
 
         spread_rows(xt_plane, xt_staged)
         spread_rows(w2_plane, w2_staged)
@@ -105,13 +105,16 @@ def tile_list_twoownboards_storeleads_one_ownpage_kernel(
         w2d_s = tile([P, R], U8, "w2d_s")
         w2d_w = tile([P, R], U32, "w2d_w")
 
-        def product(words, scales, fmt, t, board, put, name, j0=0, j1=J):
+        def multiply(words, scales, fmt, t, j0=0, j1=J):
             cols = slice(t * P, (t + 1) * P)
             acc = psum.tile([P, j1 - j0], F32, name="acc")
             nc.tensor.matmul_mx(
                 acc[:], lhsT=words[:, cols].bitcast(fmt), lhsT_scale=scales[:, cols],
                 rhs=x_w[:, j0:j1].bitcast(E5M2), rhs_scale=x_s[:, j0:j1], start=True, stop=True,
             )
+            return acc
+
+        def place(acc, board, put, name, j0=0, j1=J):
             sums = tile([P, j1 - j0], F32, name)
             nc.vector.tensor_copy(sums[:], acc[:])
             nc.scalar.activation(board[:].indirect(put[:, j0 // 16 : j1 // 16]), sums[:], COPY)
@@ -124,11 +127,11 @@ def tile_list_twoownboards_storeleads_one_ownpage_kernel(
             if j0 == 0:
                 deal(w2d_s, w2_plane, 0, 1)
             nc.vector.tensor_copy(x_w[:, j0:j1], xt_w[:].indirect(tok[:, j0 // 16 : j1 // 16]))
-            product(w2d_w, w2d_s, E4M3, 0, pv[0], put_b, "b0_%d" % j0, j0, j1)
+            place(multiply(w2d_w, w2d_s, E4M3, 0, j0, j1), pv[0], put_b, "b0_%d" % j0, j0, j1)
         deal(w2d_s, w2_plane, 1, PACK)
-        pv.append(zeroed_board(nc.gpsimd, "pv3", "w2_w"))
-        for t in range(1, PACK):
-            product(w2d_w, w2d_s, E4M3, t, pv[t], put_b, "b%d" % t)
+        pv.append(zeroed_board(nc.gpsimd, "pv3", "w2_plane"))
+        b_sums = [multiply(w2d_w, w2d_s, E4M3, t) for t in range(1, PACK)]
+        place(b_sums[0], pv[1], put_b, "b1")
 
         wt_plane = zeroed_plane(V, "wt_plane")
         load_rows(nc.sync, wt_plane, wt_scales)
@@ -140,20 +143,22 @@ def tile_list_twoownboards_storeleads_one_ownpage_kernel(
         load_rows(nc.sync, wb_s, wb_scales)
         e_s = tile([P, R], U8, "e_s", "w2d_s")
         nc.vector.tensor_copy(e_s[:], wt_plane[:].indirect(ent[:]))
+        place(b_sums[1], pv[2], put_b, "b2")
         e_w = tile([P, R], U16, "e_w", "w2d_w")
         nc.vector.tensor_copy(e_w[:], wt_w[:].indirect(ent[:]))
+        place(b_sums[2], pv[3], put_b, "b3")
         ed_s = tile([P, R], U8, "ed_s")
         ed_w = tile([P, R], U16, "ed_w")
-        pw = [zeroed_board(nc.gpsimd, "pw0", "w2_plane"), zeroed_board(nc.gpsimd, "pw1", "b1")]
+        pw = [zeroed_board(nc.gpsimd, "pw0", "b0_128"), zeroed_board(nc.gpsimd, "pw1", "b1")]
         deal(ed_s, e_s, 0, 1)
         deal(ed_w, e_w, 0, 1)
-        product(ed_w, ed_s, E2M1, 0, pw[0], put_a, "a0")
+        place(multiply(ed_w, ed_s, E2M1, 0), pw[0], put_a, "a0")
         deal(ed_s, e_s, 1, PACK)
         deal(ed_w, e_w, 1, PACK)
         pw.append(zeroed_board(nc.gpsimd, "pw2", "w2d_s"))
         pw.append(zeroed_board(nc.gpsimd, "pw3", "w2d_w"))
         for t in range(1, PACK):
-            product(ed_w, ed_s, E2M1, t, pw[t], put_a, "a%d" % t)
+            place(multiply(ed_w, ed_s, E2M1, t), pw[t], put_a, "a%d" % t)
 
         gains = tile([P, 16], F32, "gains", "a0")
         nc.sync.dma_start(gains[:, 0:PACK], sa.rearrange("(p t) o -> p (t o)", t=PACK))

@@ -2,7 +2,7 @@ from contextlib import ExitStack
 
 import concourse.mybir as mybir
 
-K, T, J, R, V, C, O, N, E = 512, 1024, 256, 512, 1024, 512, 256, 256, 512
+K, T, J, R, V, C, O, N = 512, 1024, 256, 512, 1024, 512, 256, 256
 FLOPS = 2 * K * R * J * 2 + 2 * R * N * O
 
 F32 = mybir.dt.float32
@@ -20,8 +20,10 @@ ALU = mybir.AluOpType
 P = 128
 PACK = 4
 QUADS = 4
+ENTRIES = 16
 HALF = O // 2
 ALIGN = 64
+SB_AT = 8
 
 
 def tile_list_twoownboards_storeleads_one_ownpage_kernel(
@@ -34,8 +36,8 @@ def tile_list_twoownboards_storeleads_one_ownpage_kernel(
         pool = ctx.enter_context(tc.tile_pool(name="work", bufs=1))
         psum = ctx.enter_context(tc.psum_pool(name="psum", bufs=4))
 
-        def tile(shape, dtype, name, tag=None):
-            return pool.tile(shape, dtype, name=name, tag=tag or name, align_bytes=ALIGN)
+        def tile(shape, dtype, name, after=None):
+            return pool.tile(shape, dtype, name=name, tag=after or name, align_bytes=ALIGN)
 
         def load_list(src, name):
             held = lists.tile(list(src.shape), U16, name=name)
@@ -47,15 +49,15 @@ def tile_list_twoownboards_storeleads_one_ownpage_kernel(
             nc.vector.memset(plane[:].bitcast(I32), 0)
             return plane
 
-        def load_rows(queue, plane, scales):
+        def load_rows(plane, scales):
             for q in range(QUADS):
-                queue.dma_start(plane[32 * q : 32 * q + 4, :].bitcast(I32), scales[0, 4 * q : 4 * q + 4, :].bitcast(I32))
+                nc.sync.dma_start(plane[32 * q : 32 * q + 4, :].bitcast(I32), scales[0, 4 * q : 4 * q + 4, :].bitcast(I32))
 
-        def stage_rows(queue, scales, name):
+        def stage_rows(scales, name):
             words = scales.shape[2] // 4
             staged = tile([P, 2 * words], I32, name)
             for u in range(2):
-                queue.dma_start(
+                nc.sync.dma_start(
                     staged[64 * u : 64 * u + 4, :].rearrange("r (q n) -> r q n", q=2),
                     scales[0, 8 * u : 8 * u + 8, :].bitcast(I32).rearrange("(q r) n -> r q n", r=4),
                 )
@@ -76,27 +78,31 @@ def tile_list_twoownboards_storeleads_one_ownpage_kernel(
                 src[:].rearrange("p (m t) -> p t m", t=PACK)[:, t0:t1, :],
             )
 
-        def zeroed_board(engine, name, tag=None):
-            board = tile([P, C], F32, name, tag)
+        def zeroed_board(engine, name, after=None):
+            board = tile([P, C], F32, name, after)
             engine.memset(board[:], 0.0)
             return board
 
+        wt_plane = zeroed_plane(V, "wt_plane")
         xt_plane = zeroed_plane(T, "xt_plane")
         w2_plane = zeroed_plane(R, "w2_plane")
-        xt_staged = stage_rows(nc.sync, xt_scales, "xt_staged")
-        w2_staged = stage_rows(nc.sync, w2_scales, "w2_staged")
-        tok = load_list(offs2, "tok")
+        xt_staged = stage_rows(xt_scales, "xt_staged")
+        w2_staged = stage_rows(w2_scales, "w2_staged")
+        tokens = load_list(offs2, "tokens")
         xt_w = tile([P, T], U32, "xt_w")
         nc.sync.dma_start(xt_w[:].bitcast(I32), xt_words[0].rearrange("p n t -> p (n t)").bitcast(I32))
         w2_w = tile([P, R], U32, "w2_w")
         nc.sync.dma_start(w2_w[:].bitcast(I32), w2_words[0].rearrange("p n t -> p (n t)").bitcast(I32))
         put_b = load_list(offs4, "put_b")
-        ent = load_list(offs, "ent")
+        features = load_list(offs, "features")
+        load_rows(wt_plane, wt_scales)
+        wt_w = tile([P, V], U16, "wt_w")
+        nc.sync.dma_start(wt_w[:].bitcast(I32), wt_words[0].bitcast(I32))
         put_a = load_list(offs3, "put_a")
         pick_w = load_list(offs5, "pick_w")
         pick_v = load_list(offs6, "pick_v")
         put_p = load_list(offs7, "put_p")
-        pv = [zeroed_board(nc.gpsimd if t < 1 else nc.vector, "pv%d" % t) for t in range(PACK - 1)]
+        pv = [zeroed_board(nc.gpsimd if t == 0 else nc.vector, "pv%d" % t) for t in range(PACK - 1)]
 
         spread_rows(xt_plane, xt_staged)
         spread_rows(w2_plane, w2_staged)
@@ -117,70 +123,88 @@ def tile_list_twoownboards_storeleads_one_ownpage_kernel(
         def place(acc, board, put, name, j0=0, j1=J):
             sums = tile([P, j1 - j0], F32, name)
             nc.vector.tensor_copy(sums[:], acc[:])
-            nc.scalar.activation(board[:].indirect(put[:, j0 // 16 : j1 // 16]), sums[:], COPY)
+            nc.scalar.activation(board[:].indirect(put[:, j0 // ENTRIES : j1 // ENTRIES]), sums[:], COPY)
 
         deal(w2d_w, w2_w, 0, 1, nc.scalar.copy)
         deal(w2d_w, w2_w, 1, PACK, nc.scalar.copy)
         for j0 in (0, J // 2):
             j1 = j0 + J // 2
-            nc.vector.tensor_copy(x_s[:, j0:j1], xt_plane[:].indirect(tok[:, j0 // 16 : j1 // 16]))
+            listed = tokens[:, j0 // ENTRIES : j1 // ENTRIES]
+            nc.vector.tensor_copy(x_s[:, j0:j1], xt_plane[:].indirect(listed))
             if j0 == 0:
                 deal(w2d_s, w2_plane, 0, 1)
-            nc.vector.tensor_copy(x_w[:, j0:j1], xt_w[:].indirect(tok[:, j0 // 16 : j1 // 16]))
+            nc.vector.tensor_copy(x_w[:, j0:j1], xt_w[:].indirect(listed))
             place(multiply(w2d_w, w2d_s, E4M3, 0, j0, j1), pv[0], put_b, "b0_%d" % j0, j0, j1)
         deal(w2d_s, w2_plane, 1, PACK)
-        pv.append(zeroed_board(nc.gpsimd, "pv3", "w2_plane"))
+        pv.append(zeroed_board(nc.gpsimd, "pv3", after="w2_plane"))
         b_sums = [multiply(w2d_w, w2d_s, E4M3, t) for t in range(1, PACK)]
         place(b_sums[0], pv[1], put_b, "b1")
 
-        wt_plane = zeroed_plane(V, "wt_plane")
-        load_rows(nc.sync, wt_plane, wt_scales)
-        wt_w = tile([P, V], U16, "wt_w")
-        nc.sync.dma_start(wt_w[:].bitcast(I32), wt_words[0].bitcast(I32))
         wb_s = zeroed_plane(N, "wb_s")
         wb_w = tile([P, N], U16, "wb_w")
         nc.sync.dma_start(wb_w[:].bitcast(I32), wb_words[0].bitcast(I32))
-        load_rows(nc.sync, wb_s, wb_scales)
-        e_s = tile([P, R], U8, "e_s", "w2d_s")
-        nc.vector.tensor_copy(e_s[:], wt_plane[:].indirect(ent[:]))
+        load_rows(wb_s, wb_scales)
+
+        e_s = tile([P, R], U8, "e_s", after="w2d_s")
+        nc.vector.tensor_copy(e_s[:], wt_plane[:].indirect(features[:]))
         place(b_sums[1], pv[2], put_b, "b2")
-        e_w = tile([P, R], U16, "e_w", "w2d_w")
-        nc.vector.tensor_copy(e_w[:], wt_w[:].indirect(ent[:]))
+        e_w = tile([P, R], U16, "e_w", after="w2d_w")
+        nc.vector.tensor_copy(e_w[:], wt_w[:].indirect(features[:]))
         place(b_sums[2], pv[3], put_b, "b3")
         ed_s = tile([P, R], U8, "ed_s")
         ed_w = tile([P, R], U16, "ed_w")
-        pw = [zeroed_board(nc.gpsimd, "pw0", "b0_128"), zeroed_board(nc.gpsimd, "pw1", "b1")]
+        pw = [zeroed_board(nc.gpsimd, "pw0", after="b0_%d" % (J // 2)), zeroed_board(nc.gpsimd, "pw1", after="b1")]
         deal(ed_s, e_s, 0, 1)
         deal(ed_w, e_w, 0, 1)
         place(multiply(ed_w, ed_s, E2M1, 0), pw[0], put_a, "a0")
         deal(ed_s, e_s, 1, PACK)
         deal(ed_w, e_w, 1, PACK)
-        pw.append(zeroed_board(nc.gpsimd, "pw2", "w2d_s"))
-        pw.append(zeroed_board(nc.gpsimd, "pw3", "w2d_w"))
+        pw.append(zeroed_board(nc.gpsimd, "pw2", after="w2d_s"))
+        pw.append(zeroed_board(nc.gpsimd, "pw3", after="w2d_w"))
         for t in range(1, PACK):
             place(multiply(ed_w, ed_s, E2M1, t), pw[t], put_a, "a%d" % t)
 
-        gains = tile([P, 16], F32, "gains", "a0")
+        gains = tile([P, 2 * SB_AT], F32, "gains", after="a0")
         nc.sync.dma_start(gains[:, 0:PACK], sa.rearrange("(p t) o -> p (t o)", t=PACK))
-        nc.sync.dma_start(gains[:, 8 : 8 + PACK], sb.rearrange("(p t) o -> p (t o)", t=PACK))
-        pages = [zeroed_board(nc.gpsimd, "page%d" % c, "a%d" % (c + 1)) for c in range(N // P)]
+        nc.sync.dma_start(gains[:, SB_AT : SB_AT + PACK], sb.rearrange("(p t) o -> p (t o)", t=PACK))
+        pages = [zeroed_board(nc.gpsimd, "page%d" % c, after="a%d" % (c + 1)) for c in range(N // P)]
 
-        def hidden(h):
-            cols = slice(h * HALF // 16, (h + 1) * HALF // 16)
+        def second_stage(h):
             gw = tile([P, PACK, HALF], F32, "gw%d" % h)
             gv = tile([P, PACK, HALF], F32, "gv%d" % h)
             diff = tile([P, PACK, HALF], F32, "diff%d" % h)
             hid = tile([P, HALF, PACK], BF16, "hid%d" % h)
-            for t in range(PACK):
-                nc.scalar.activation(gv[:, t, :], pv[t][:].indirect(pick_v[:, cols]), COPY, scale=gains[:, 8 + t : 9 + t])
-                nc.scalar.activation(gw[:, t, :], pw[t][:].indirect(pick_w[:, cols]), COPY, scale=gains[:, t : t + 1])
-                nc.vector.tensor_tensor(diff[:, t, :], gw[:, t, :], gv[:, t, :], ALU.subtract)
-                if t % 2 == 1:
-                    pair = diff[:, t - 1 : t + 1, :].rearrange("p t o -> p o t")
-                    nc.vector.scalar_tensor_tensor(hid[:, :, t - 1 : t + 1], pair, -1.0, pair, ALU.mult, ALU.max)
             h_w = tile([P, HALF], U32, "h_w%d" % h)
             h_s = tile([P, HALF], U8, "h_s%d" % h)
-            nc.vector.quantize_mx(h_w[:].bitcast(E4M3), h_s[:], hid[:].rearrange("p o t -> p (o t)"))
+            whole = [(0, HALF)]
+            last = whole if h == 0 else [(0, HALF // 2), (HALF // 2, HALF)]
+
+            def fetch(dst, board, pick, gain, o0, o1):
+                listed = pick[:, (h * HALF + o0) // ENTRIES : (h * HALF + o1) // ENTRIES]
+                nc.scalar.activation(dst[:, o0:o1], board[:].indirect(listed), COPY, scale=gain)
+
+            def subtract(t0, t1, o0, o1):
+                nc.vector.tensor_tensor(diff[:, t0:t1, o0:o1], gw[:, t0:t1, o0:o1], gv[:, t0:t1, o0:o1], ALU.subtract)
+
+            def magnitude(t0, o0, o1):
+                pair = diff[:, t0 : t0 + 2, o0:o1].rearrange("p t o -> p o t")
+                nc.vector.scalar_tensor_tensor(hid[:, o0:o1, t0 : t0 + 2], pair, -1.0, pair, ALU.mult, ALU.max)
+
+            for t in range(PACK):
+                fetch(gv[:, t, :], pv[t], pick_v, gains[:, SB_AT + t : SB_AT + t + 1], 0, HALF)
+                for o0, o1 in last if t == PACK - 1 else whole:
+                    fetch(gw[:, t, :], pw[t], pick_w, gains[:, t : t + 1], o0, o1)
+            subtract(0, 2, 0, HALF)
+            magnitude(0, 0, HALF)
+            subtract(2, 3, 0, HALF)
+            for o0, o1 in last:
+                subtract(3, 4, o0, o1)
+            for o0, o1 in last:
+                magnitude(2, o0, o1)
+            for o0, o1 in last:
+                nc.vector.quantize_mx(
+                    h_w[:, o0:o1].bitcast(E4M3), h_s[:, o0:o1], hid[:, o0:o1, :].rearrange("p o t -> p (o t)")
+                )
             results = []
             for c in range(N // P):
                 acc = psum.tile([P, HALF], F32, name="acc_p")
@@ -188,14 +212,16 @@ def tile_list_twoownboards_storeleads_one_ownpage_kernel(
                     acc[:], lhsT=wb_w[:, c * P : (c + 1) * P].bitcast(E2M1), lhsT_scale=wb_s[:, c * P : (c + 1) * P],
                     rhs=h_w[:].bitcast(E4M3), rhs_scale=h_s[:], start=True, stop=True,
                 )
-                sums = tile([P, HALF], F32, "p%d%d" % (h, c))
-                nc.vector.tensor_copy(sums[:], acc[:])
-                results.append(sums)
+                results.append(acc)
             return results
 
-        halves = [hidden(h) for h in range(2)]
-        for h in range(2):
+        halves = [second_stage(h) for h in range(2)]
+        for h, copy in enumerate((nc.scalar.copy, nc.vector.tensor_copy)):
+            p_sums = [tile([P, HALF], F32, "p%d%d" % (h, c)) for c in range(N // P)]
+            listed = put_p[:, h * HALF // ENTRIES : (h + 1) * HALF // ENTRIES]
             for c in range(N // P):
-                nc.scalar.activation(pages[c][:].indirect(put_p[:, h * HALF // 16 : (h + 1) * HALF // 16]), halves[h][c][:], COPY)
+                copy(p_sums[c][:], halves[h][c][:])
+            for c in range(N // P):
+                nc.scalar.activation(pages[c][:].indirect(listed), p_sums[c][:], COPY)
         for c in range(N // P):
             nc.sync.dma_start(out[c * P : (c + 1) * P, :], pages[c][:])

from contextlib import ExitStack

import concourse.mybir as mybir

K, T, J, R, V, C, O, N = 512, 1024, 256, 512, 1024, 512, 256, 256
FLOPS = 2 * K * R * J * 2 + 2 * R * N * O

F32 = mybir.dt.float32
BF16 = mybir.dt.bfloat16
I32 = mybir.dt.int32
U32 = mybir.dt.uint32
U16 = mybir.dt.uint16
U8 = mybir.dt.uint8
E4M3 = mybir.dt.float8_e4m3fn_x4
E5M2 = mybir.dt.float8_e5m2_x4
E2M1 = mybir.dt.float4_e2m1fn_x4
COPY = mybir.ActivationFunctionType.Copy
ALU = mybir.AluOpType

P = 128
PACK = 4
QUADS = 4
ENTRIES = 16
HALF = O // 2
ALIGN = 64
SB_AT = 8


def tile_list_twoownboards_storeleads_one_ownpage_kernel(
    tc, xt_words, xt_scales, wt_words, wt_scales, w2_words, w2_scales, sa, sb, wb_words, wb_scales,
    offs, offs2, offs3, offs4, offs5, offs6, offs7, out,
):
    nc = tc.nc
    with ExitStack() as ctx:
        lists = ctx.enter_context(tc.tile_pool(name="lists", bufs=1))
        pool = ctx.enter_context(tc.tile_pool(name="work", bufs=1))
        psum = ctx.enter_context(tc.psum_pool(name="psum", bufs=4))

        def tile(shape, dtype, name, after=None):
            return pool.tile(shape, dtype, name=name, tag=after or name, align_bytes=ALIGN)

        def load_list(src, name):
            held = lists.tile(list(src.shape), U16, name=name)
            nc.sync.dma_start(held[:], src)
            return held

        def zeroed_plane(width, name):
            plane = tile([P, width], U8, name)
            nc.vector.memset(plane[:].bitcast(I32), 0)
            return plane

        def load_rows(plane, scales):
            for q in range(QUADS):
                nc.sync.dma_start(plane[32 * q : 32 * q + 4, :].bitcast(I32), scales[0, 4 * q : 4 * q + 4, :].bitcast(I32))

        def stage_rows(scales, name):
            words = scales.shape[2] // 4
            staged = tile([P, 2 * words], I32, name)
            for u in range(2):
                nc.sync.dma_start(
                    staged[64 * u : 64 * u + 4, :].rearrange("r (q n) -> r q n", q=2),
                    scales[0, 8 * u : 8 * u + 8, :].bitcast(I32).rearrange("(q r) n -> r q n", r=4),
                )
            return staged

        def spread_rows(plane, staged):
            words = staged.shape[1] // 2
            for q in range(QUADS):
                first = 64 * (q // 2)
                nc.vector.tensor_copy(
                    plane[32 * q : 32 * q + 4, :].bitcast(I32),
                    staged[first : first + 4, (q % 2) * words : (q % 2 + 1) * words],
                )

        def deal(dst, src, t0, t1, copy=nc.vector.tensor_copy):
            copy(
                dst[:, t0 * P : t1 * P].rearrange("p (t m) -> p t m", m=P),
                src[:].rearrange("p (m t) -> p t m", t=PACK)[:, t0:t1, :],
            )

        def zeroed_board(engine, name, after=None):
            board = tile([P, C], F32, name, after)
            engine.memset(board[:], 0.0)
            return board

        wt_plane = zeroed_plane(V, "wt_plane")
        xt_plane = zeroed_plane(T, "xt_plane")
        w2_plane = zeroed_plane(R, "w2_plane")
        xt_staged = stage_rows(xt_scales, "xt_staged")
        w2_staged = stage_rows(w2_scales, "w2_staged")
        tokens = load_list(offs2, "tokens")
        xt_w = tile([P, T], U32, "xt_w")
        nc.sync.dma_start(xt_w[:].bitcast(I32), xt_words[0].rearrange("p n t -> p (n t)").bitcast(I32))
        w2_w = tile([P, R], U32, "w2_w")
        nc.sync.dma_start(w2_w[:].bitcast(I32), w2_words[0].rearrange("p n t -> p (n t)").bitcast(I32))
        put_b = load_list(offs4, "put_b")
        features = load_list(offs, "features")
        load_rows(wt_plane, wt_scales)
        wt_w = tile([P, V], U16, "wt_w")
        nc.sync.dma_start(wt_w[:].bitcast(I32), wt_words[0].bitcast(I32))
        put_a = load_list(offs3, "put_a")
        pick_w = load_list(offs5, "pick_w")
        pick_v = load_list(offs6, "pick_v")
        put_p = load_list(offs7, "put_p")
        pv = [zeroed_board(nc.gpsimd if t == 0 else nc.vector, "pv%d" % t) for t in range(PACK - 1)]

        spread_rows(xt_plane, xt_staged)
        spread_rows(w2_plane, w2_staged)
        x_s = tile([P, J], U8, "x_s")
        x_w = tile([P, J], U32, "x_w")
        w2d_s = tile([P, R], U8, "w2d_s")
        w2d_w = tile([P, R], U32, "w2d_w")

        def multiply(words, scales, fmt, t, j0=0, j1=J):
            cols = slice(t * P, (t + 1) * P)
            acc = psum.tile([P, j1 - j0], F32, name="acc")
            nc.tensor.matmul_mx(
                acc[:], lhsT=words[:, cols].bitcast(fmt), lhsT_scale=scales[:, cols],
                rhs=x_w[:, j0:j1].bitcast(E5M2), rhs_scale=x_s[:, j0:j1], start=True, stop=True,
            )
            return acc

        def place(acc, board, put, name, j0=0, j1=J):
            sums = tile([P, j1 - j0], F32, name)
            nc.vector.tensor_copy(sums[:], acc[:])
            nc.scalar.activation(board[:].indirect(put[:, j0 // ENTRIES : j1 // ENTRIES]), sums[:], COPY)

        deal(w2d_w, w2_w, 0, 1, nc.scalar.copy)
        deal(w2d_w, w2_w, 1, PACK, nc.scalar.copy)
        for j0 in (0, J // 2):
            j1 = j0 + J // 2
            listed = tokens[:, j0 // ENTRIES : j1 // ENTRIES]
            nc.vector.tensor_copy(x_s[:, j0:j1], xt_plane[:].indirect(listed))
            if j0 == 0:
                deal(w2d_s, w2_plane, 0, 1)
            nc.vector.tensor_copy(x_w[:, j0:j1], xt_w[:].indirect(listed))
            place(multiply(w2d_w, w2d_s, E4M3, 0, j0, j1), pv[0], put_b, "b0_%d" % j0, j0, j1)
        deal(w2d_s, w2_plane, 1, PACK)
        pv.append(zeroed_board(nc.gpsimd, "pv3", after="w2_plane"))
        b_sums = [multiply(w2d_w, w2d_s, E4M3, t) for t in range(1, PACK)]
        place(b_sums[0], pv[1], put_b, "b1")

        wb_s = zeroed_plane(N, "wb_s")
        wb_w = tile([P, N], U16, "wb_w")
        nc.sync.dma_start(wb_w[:].bitcast(I32), wb_words[0].bitcast(I32))
        load_rows(wb_s, wb_scales)

        e_s = tile([P, R], U8, "e_s", after="w2d_s")
        nc.vector.tensor_copy(e_s[:], wt_plane[:].indirect(features[:]))
        place(b_sums[1], pv[2], put_b, "b2")
        e_w = tile([P, R], U16, "e_w", after="w2d_w")
        nc.vector.tensor_copy(e_w[:], wt_w[:].indirect(features[:]))
        place(b_sums[2], pv[3], put_b, "b3")
        ed_s = tile([P, R], U8, "ed_s")
        ed_w = tile([P, R], U16, "ed_w")
        pw = [zeroed_board(nc.gpsimd, "pw0", after="b0_%d" % (J // 2)), zeroed_board(nc.gpsimd, "pw1", after="b1")]
        deal(ed_s, e_s, 0, 1)
        deal(ed_w, e_w, 0, 1)
        place(multiply(ed_w, ed_s, E2M1, 0), pw[0], put_a, "a0")
        deal(ed_s, e_s, 1, PACK)
        deal(ed_w, e_w, 1, PACK)
        pw.append(zeroed_board(nc.gpsimd, "pw2", after="w2d_s"))
        pw.append(zeroed_board(nc.gpsimd, "pw3", after="w2d_w"))
        for t in range(1, PACK):
            place(multiply(ed_w, ed_s, E2M1, t), pw[t], put_a, "a%d" % t)

        gains = tile([P, 2 * SB_AT], F32, "gains", after="a0")
        nc.sync.dma_start(gains[:, 0:PACK], sa.rearrange("(p t) o -> p (t o)", t=PACK))
        nc.sync.dma_start(gains[:, SB_AT : SB_AT + PACK], sb.rearrange("(p t) o -> p (t o)", t=PACK))
        pages = [zeroed_board(nc.gpsimd, "page%d" % c, after="a%d" % (c + 1)) for c in range(N // P)]

        def second_stage(h):
            gw = tile([P, PACK, HALF], F32, "gw%d" % h)
            gv = tile([P, PACK, HALF], F32, "gv%d" % h)
            diff = tile([P, PACK, HALF], F32, "diff%d" % h)
            hid = tile([P, HALF, PACK], BF16, "hid%d" % h)
            h_w = tile([P, HALF], U32, "h_w%d" % h)
            h_s = tile([P, HALF], U8, "h_s%d" % h)
            whole = [(0, HALF)]
            last = whole if h == 0 else [(0, HALF // 2), (HALF // 2, HALF)]

            def fetch(dst, board, pick, gain, o0, o1):
                listed = pick[:, (h * HALF + o0) // ENTRIES : (h * HALF + o1) // ENTRIES]
                nc.scalar.activation(dst[:, o0:o1], board[:].indirect(listed), COPY, scale=gain)

            def subtract(t0, t1, o0, o1):
                nc.vector.tensor_tensor(diff[:, t0:t1, o0:o1], gw[:, t0:t1, o0:o1], gv[:, t0:t1, o0:o1], ALU.subtract)

            def magnitude(t0, o0, o1):
                pair = diff[:, t0 : t0 + 2, o0:o1].rearrange("p t o -> p o t")
                nc.vector.scalar_tensor_tensor(hid[:, o0:o1, t0 : t0 + 2], pair, -1.0, pair, ALU.mult, ALU.max)

            for t in range(PACK):
                fetch(gv[:, t, :], pv[t], pick_v, gains[:, SB_AT + t : SB_AT + t + 1], 0, HALF)
                for o0, o1 in last if t == PACK - 1 else whole:
                    fetch(gw[:, t, :], pw[t], pick_w, gains[:, t : t + 1], o0, o1)
            subtract(0, 2, 0, HALF)
            magnitude(0, 0, HALF)
            subtract(2, 3, 0, HALF)
            for o0, o1 in last:
                subtract(3, 4, o0, o1)
            for o0, o1 in last:
                magnitude(2, o0, o1)
            for o0, o1 in last:
                nc.vector.quantize_mx(
                    h_w[:, o0:o1].bitcast(E4M3), h_s[:, o0:o1], hid[:, o0:o1, :].rearrange("p o t -> p (o t)")
                )
            results = []
            for c in range(N // P):
                acc = psum.tile([P, HALF], F32, name="acc_p")
                nc.tensor.matmul_mx(
                    acc[:], lhsT=wb_w[:, c * P : (c + 1) * P].bitcast(E2M1), lhsT_scale=wb_s[:, c * P : (c + 1) * P],
                    rhs=h_w[:].bitcast(E4M3), rhs_scale=h_s[:], start=True, stop=True,
                )
                results.append(acc)
            return results

        halves = [second_stage(h) for h in range(2)]
        for h, copy in enumerate((nc.scalar.copy, nc.vector.tensor_copy)):
            p_sums = [tile([P, HALF], F32, "p%d%d" % (h, c)) for c in range(N // P)]
            listed = put_p[:, h * HALF // ENTRIES : (h + 1) * HALF // ENTRIES]
            for c in range(N // P):
                copy(p_sums[c][:], halves[h][c][:])
            for c in range(N // P):
                nc.scalar.activation(pages[c][:].indirect(listed), p_sums[c][:], COPY)
        for c in range(N // P):
            nc.sync.dma_start(out[c * P : (c + 1) * P, :], pages[c][:])
